import numpy as np, ml_dtypes
CORES = [136,8,152,24,168,40,184,56,200,72,216,88,232,104,248,120]
N = 16
G1 = [0,1,2,3,4,5,6,7,8,9,10,11,12,13,14,15]
G2 = [0,2,4,6,8,10,12,14]
def setup_inputs(rng):
    return {"x1": rng.standard_normal((N, 128, 1024), dtype=np.float32), "x2": rng.standard_normal((N, 128, 64), dtype=np.float32).astype(ml_dtypes.bfloat16)}
def reference(x1, x2):
    out = {}
    y = np.full((N, 128, 1024), np.nan, x1.dtype)
    s = x1[G1].sum(axis=0, dtype=np.float64).astype(x1.dtype)
    for r in G1:
        y[r] = s
    out["y1"] = y
    y = np.full((N, 128, 64), np.nan, x2.dtype)
    for i, r in enumerate(G2):
        y[r] = np.concatenate([x2[s][:, 8 * i:8 * i + 8] for s in G2], axis=1)
    out["y2"] = y
    return out

@@ -1,0 +1,173 @@
+from concourse.bass import DstId, RemoteDMATransfer
+
+WORLD = 256
+P = 128
+M = 16
+COLS = 1024
+
+LANES = (
+    (16, (("own", 1, 0, 0), ("own", 1, 0, 1)), ("own", 1, 0, 0)),
+    (16, (("own", 0, 1, 0), ("own", 0, 1, 1)), ("mate", 0, 1, 0)),
+    (16, (("own", 1, 1, 0), ("own", 1, 1, 1)), ("mate", 1, 1, 0)),
+    (16, (), ("own", 0, 0, 0)),
+)
+NL = len(LANES)
+
+SCRATCH = {
+    "xs2": ("sbuf", [P, 64], "bfloat16"),
+    "land2": ("sbuf", [P, 64], "bfloat16"),
+}
+SEMAPHORES = ["rel", "got", "sent", "l2", "l2o", "a2", "sty2"]
+for _l in range(NL):
+    SCRATCH["s%d" % _l] = ("dram", [M, P, LANES[_l][0]], "float32")
+    SCRATCH["r%d" % _l] = ("dram", [M, P, LANES[_l][0]], "float32")
+    SEMAPHORES += ["ld%d" % _l, "arr%d" % _l, "st%d" % _l]
+
+
+def _engines(m):
+    out = []
+    while m:
+        out.append(m & -m)
+        m &= m - 1
+    return out
+
+
+def _pick(topo, r, sel):
+    where, far, port, n = sel
+    own = [c for c in range(WORLD) if c != r and topo.host(c) == topo.host(r) and topo.chip(c) == topo.chip(r)]
+    mate = [c for c in range(WORLD) if topo.mates(c, r)]
+    pool, across = (own, mate[0]) if where == "own" else (mate, r)
+    return [c for c in pool if (topo.die(c) != topo.die(r)) == bool(far) and topo.may_write(c, across) == bool(port)][n]
+
+
+def _wires(T, topo):
+    members = [T.cores[r] for r in T.tables["G1"]]
+    wires = []
+    for r in members:
+        wires.append([([_pick(topo, r, s) for s in fwd] or [r], _pick(topo, r, red)) for (_w, fwd, red) in LANES])
+    return members, wires
+
+
+def _share(k, n, f):
+    ring = [(k + t) % M for t in range(M)]
+    return ring[f * M // n:(f + 1) * M // n]
+
+
+def _fan(g, core, topo, items, local_sem):
+    batch, used, n = [], 0, 0
+    for dst, s_ap, d_ap, sem in items:
+        free = [e for e in _engines(topo.mask(core, dst)) if not e & used]
+        if not free:
+            g.remote_dma_fused(batch, local_sem=local_sem)
+            batch, used = [], 0
+            free = _engines(topo.mask(core, dst))
+        used |= free[-1]
+        rid, pid = topo.addr(dst, core)
+        batch.append(RemoteDMATransfer(dst_ids=[DstId(rid=rid, pnc=pid)], dma_engine_mask=free[-1], remote_sem=sem,
+                                       src=s_ap, dst=d_ap))
+        n += 1
+    if batch:
+        g.remote_dma_fused(batch, local_sem=local_sem)
+    return n
+
+
+def _scatter(g, core, T, topo, wires, k, l, pieces):
+    s, r = T["s%d" % l], T["r%d" % l]
+    return _fan(g, core, topo, [(wires[j][l][1], s[j], r[k], T.sem.got) for j in pieces if wires[j][l][1] != core],
+                T.sem.sent)
+
+
+def _fold_mask(topo, red, members):
+    m = topo.mask(red, members[0])
+    for c in members:
+        m &= topo.mask(red, c)
+    return m
+
+
+def _helper(g, core, T, topo, members, wires):
+    S = T.sem
+    sent = 0
+    busy = False
+    for k in range(M):
+        for l in range(NL):
+            snd, red = wires[k][l]
+            if core in snd and core != members[k]:
+                mine = _share(k, len(snd), snd.index(core))
+                g.wait_ge(S.rel, len(mine))
+                sent += _scatter(g, core, T, topo, wires, k, l, mine)
+                busy = True
+    for k in range(M):
+        for l in range(NL):
+            if wires[k][l][1] != core:
+                continue
+            srcs, n_in = [], 0
+            for i in range(M):
+                snd = wires[i][l][0]
+                frm = [c for f, c in enumerate(snd) if k in _share(i, len(snd), f)][0]
+                if frm == core:
+                    srcs.append(T["s%d" % l][k])
+                else:
+                    srcs.append(T["r%d" % l][i])
+                    n_in += 1
+            g.wait_ge(S.got, n_in)
+            mask = _fold_mask(topo, core, members)
+            ids = [DstId(rid=topo.addr(c, core)[0], pnc=topo.addr(c, core)[1]) for c in members]
+            g.remote_dma_fused([RemoteDMATransfer(dst_ids=ids, dma_engine_mask=mask, remote_sem=S["arr%d" % l], srcs=srcs,
+                                                  dsts=[T["r%d" % l][k] for _c in members], alu_op=1)], local_sem=S.sent)
+            sent += len(_engines(mask))
+            busy = True
+    if busy:
+        g.wait_ge(S.sent, sent)
+
+
+def _rank(g, core, T, topo, members, wires):
+    S = T.sem
+    k = members.index(core)
+    queues = (g.sync, g.scalar)
+    group2 = [T.cores[r] for r in T.tables["G2"]]
+    in2 = core in group2
+    span, row = [], 0
+    for l in range(NL):
+        n = M * P * LANES[l][0] // COLS
+        span.append((row, row + n))
+        queues[l % 2].dma_start(T["s%d" % l][:], T.x1[row:row + n, :]).then_inc(S["ld%d" % l], 16)
+        row += n
+    if in2:
+        me = group2.index(core)
+        b = T.x2.shape[1] // len(group2)
+        g.sync.dma_start(T.xs2[:], T.x2[:]).then_inc(S.l2, 16)
+        g.scalar.dma_start(T.land2[:, b * me:b * me + b], T.x2[:, b * me:b * me + b]).then_inc(S.l2o, 16)
+    sent = 0
+    for l in range(NL):
+        snd = wires[k][l][0]
+        g.wait_ge(S["ld%d" % l], 16)
+        if snd == [core]:
+            sent += _scatter(g, core, T, topo, wires, k, l, _share(k, 1, 0))
+        else:
+            s = T["s%d" % l]
+            sent += _fan(g, core, topo, [(c, s[j], s[j], S.rel) for f, c in enumerate(snd) for j in _share(k, len(snd), f)],
+                         S.sent)
+    if in2:
+        g.wait_ge(S.l2, 16)
+        sent += _fan(g, core, topo, [(c, T.xs2[:, b * j:b * j + b], T.land2[:, b * me:b * me + b], S.a2)
+                                     for j, c in enumerate(group2) if c != core], S.sent)
+    for l in range(NL):
+        q = queues[l % 2]
+        q.wait_ge(S["arr%d" % l], sum(len(_engines(_fold_mask(topo, wires[j][l][1], members))) for j in range(M)))
+        q.dma_start(T.y1[span[l][0]:span[l][1], :], T["r%d" % l][:]).then_inc(S["st%d" % l], 16)
+    if in2:
+        g.wait_ge(S.l2o, 16)
+        g.wait_ge(S.a2, len(group2) - 1)
+        g.dma_start(T.y2[:], T.land2[:]).then_inc(S.sty2, 16)
+        g.wait_ge(S.sty2, 16)
+    g.wait_ge(S.sent, sent)
+    for l in range(NL):
+        queues[l % 2].wait_ge(S["st%d" % l], 16)
+
+
+def rank_program(g, core, T, topo):
+    members, wires = _wires(T, topo)
+    if core in members:
+        _rank(g, core, T, topo, members, wires)
+    else:
+        _helper(g, core, T, topo, members, wires)

@@ -9,9 +9,10 @@ LANES = (
     (16, (("own", 1, 0, 0), ("own", 1, 0, 1)), ("own", 1, 0, 0)),
     (16, (("own", 0, 1, 0), ("own", 0, 1, 1)), ("mate", 0, 1, 0)),
     (16, (("own", 1, 1, 0), ("own", 1, 1, 1)), ("mate", 1, 1, 0)),
-    (16, (), ("own", 0, 0, 0)),
+    (16, ("self",), ("own", 0, 0, 0)),
 )
 NL = len(LANES)
+STORES = ((0, 2), (1, 3))
 
 SCRATCH = {
     "xs2": ("sbuf", [P, 64], "bfloat16"),
@@ -33,6 +34,8 @@ def _engines(m):
 
 
 def _pick(topo, r, sel):
+    if sel == "self":
+        return r
     where, far, port, n = sel
     own = [c for c in range(WORLD) if c != r and topo.host(c) == topo.host(r) and topo.chip(c) == topo.chip(r)]
     mate = [c for c in range(WORLD) if topo.mates(c, r)]
@@ -44,7 +47,7 @@ def _wires(T, topo):
     members = [T.cores[r] for r in T.tables["G1"]]
     wires = []
     for r in members:
-        wires.append([([_pick(topo, r, s) for s in fwd] or [r], _pick(topo, r, red)) for (_w, fwd, red) in LANES])
+        wires.append([([_pick(topo, r, s) for s in snd], _pick(topo, r, red)) for (_w, snd, red) in LANES])
     return members, wires
 
 
@@ -71,10 +74,9 @@ def _fan(g, core, topo, items, local_sem):
     return n
 
 
-def _scatter(g, core, T, topo, wires, k, l, pieces):
+def _to_reducers(core, T, wires, k, l, pieces):
     s, r = T["s%d" % l], T["r%d" % l]
-    return _fan(g, core, topo, [(wires[j][l][1], s[j], r[k], T.sem.got) for j in pieces if wires[j][l][1] != core],
-                T.sem.sent)
+    return [(wires[j][l][1], s[j], r[k], T.sem.got) for j in pieces if wires[j][l][1] != core]
 
 
 def _fold_mask(topo, red, members):
@@ -91,10 +93,10 @@ def _helper(g, core, T, topo, members, wires):
     for k in range(M):
         for l in range(NL):
             snd, red = wires[k][l]
-            if core in snd and core != members[k]:
+            if core in snd:
                 mine = _share(k, len(snd), snd.index(core))
                 g.wait_ge(S.rel, len(mine))
-                sent += _scatter(g, core, T, topo, wires, k, l, mine)
+                sent += _fan(g, core, topo, _to_reducers(core, T, wires, k, l, mine), S.sent)
                 busy = True
     for k in range(M):
         for l in range(NL):
@@ -111,9 +113,10 @@ def _helper(g, core, T, topo, members, wires):
                     n_in += 1
             g.wait_ge(S.got, n_in)
             mask = _fold_mask(topo, core, members)
-            ids = [DstId(rid=topo.addr(c, core)[0], pnc=topo.addr(c, core)[1]) for c in members]
+            ring = [members[(k + 1 + t) % M] for t in range(M)]
+            ids = [DstId(rid=topo.addr(c, core)[0], pnc=topo.addr(c, core)[1]) for c in ring]
             g.remote_dma_fused([RemoteDMATransfer(dst_ids=ids, dma_engine_mask=mask, remote_sem=S["arr%d" % l], srcs=srcs,
-                                                  dsts=[T["r%d" % l][k] for _c in members], alu_op=1)], local_sem=S.sent)
+                                                  dsts=[T["r%d" % l][k] for _c in ring], alu_op=1)], local_sem=S.sent)
             sent += len(_engines(mask))
             busy = True
     if busy:
@@ -126,6 +129,8 @@ def _rank(g, core, T, topo, members, wires):
     queues = (g.sync, g.scalar)
     group2 = [T.cores[r] for r in T.tables["G2"]]
     in2 = core in group2
+    me = group2.index(core) if in2 else 0
+    b = T.x2.shape[1] // len(group2)
     span, row = [], 0
     for l in range(NL):
         n = M * P * LANES[l][0] // COLS
@@ -133,36 +138,35 @@ def _rank(g, core, T, topo, members, wires):
         queues[l % 2].dma_start(T["s%d" % l][:], T.x1[row:row + n, :]).then_inc(S["ld%d" % l], 16)
         row += n
     if in2:
-        me = group2.index(core)
-        b = T.x2.shape[1] // len(group2)
         g.sync.dma_start(T.xs2[:], T.x2[:]).then_inc(S.l2, 16)
         g.scalar.dma_start(T.land2[:, b * me:b * me + b], T.x2[:, b * me:b * me + b]).then_inc(S.l2o, 16)
     sent = 0
     for l in range(NL):
         snd = wires[k][l][0]
+        s = T["s%d" % l]
+        items = []
+        for f, c in enumerate(snd):
+            mine = _share(k, len(snd), f)
+            items += _to_reducers(core, T, wires, k, l, mine) if c == core else [(c, s[j], s[j], S.rel) for j in mine]
         g.wait_ge(S["ld%d" % l], 16)
-        if snd == [core]:
-            sent += _scatter(g, core, T, topo, wires, k, l, _share(k, 1, 0))
-        else:
-            s = T["s%d" % l]
-            sent += _fan(g, core, topo, [(c, s[j], s[j], S.rel) for f, c in enumerate(snd) for j in _share(k, len(snd), f)],
-                         S.sent)
+        sent += _fan(g, core, topo, items, S.sent)
     if in2:
         g.wait_ge(S.l2, 16)
         sent += _fan(g, core, topo, [(c, T.xs2[:, b * j:b * j + b], T.land2[:, b * me:b * me + b], S.a2)
                                      for j, c in enumerate(group2) if c != core], S.sent)
-    for l in range(NL):
-        q = queues[l % 2]
-        q.wait_ge(S["arr%d" % l], sum(len(_engines(_fold_mask(topo, wires[j][l][1], members))) for j in range(M)))
-        q.dma_start(T.y1[span[l][0]:span[l][1], :], T["r%d" % l][:]).then_inc(S["st%d" % l], 16)
+    for q, lanes in zip(queues, STORES):
+        for l in lanes:
+            q.wait_ge(S["arr%d" % l], sum(len(_engines(_fold_mask(topo, wires[j][l][1], members))) for j in range(M)))
+            q.dma_start(T.y1[span[l][0]:span[l][1], :], T["r%d" % l][:]).then_inc(S["st%d" % l], 16)
     if in2:
         g.wait_ge(S.l2o, 16)
         g.wait_ge(S.a2, len(group2) - 1)
         g.dma_start(T.y2[:], T.land2[:]).then_inc(S.sty2, 16)
         g.wait_ge(S.sty2, 16)
     g.wait_ge(S.sent, sent)
-    for l in range(NL):
-        queues[l % 2].wait_ge(S["st%d" % l], 16)
+    for q, lanes in zip(queues, STORES):
+        for l in lanes:
+            q.wait_ge(S["st%d" % l], 16)
 
 
 def rank_program(g, core, T, topo):

from concourse.bass import DstId, RemoteDMATransfer

WORLD = 256
P = 128
M = 16
COLS = 1024

LANES = (
    (16, (("own", 1, 0, 0), ("own", 1, 0, 1)), ("own", 1, 0, 0)),
    (16, (("own", 0, 1, 0), ("own", 0, 1, 1)), ("mate", 0, 1, 0)),
    (16, (("own", 1, 1, 0), ("own", 1, 1, 1)), ("mate", 1, 1, 0)),
    (16, ("self",), ("own", 0, 0, 0)),
)
NL = len(LANES)
STORES = ((0, 2), (1, 3))

SCRATCH = {
    "xs2": ("sbuf", [P, 64], "bfloat16"),
    "land2": ("sbuf", [P, 64], "bfloat16"),
}
SEMAPHORES = ["rel", "got", "sent", "l2", "l2o", "a2", "sty2"]
for _l in range(NL):
    SCRATCH["s%d" % _l] = ("dram", [M, P, LANES[_l][0]], "float32")
    SCRATCH["r%d" % _l] = ("dram", [M, P, LANES[_l][0]], "float32")
    SEMAPHORES += ["ld%d" % _l, "arr%d" % _l, "st%d" % _l]


def _engines(m):
    out = []
    while m:
        out.append(m & -m)
        m &= m - 1
    return out


def _pick(topo, r, sel):
    if sel == "self":
        return r
    where, far, port, n = sel
    own = [c for c in range(WORLD) if c != r and topo.host(c) == topo.host(r) and topo.chip(c) == topo.chip(r)]
    mate = [c for c in range(WORLD) if topo.mates(c, r)]
    pool, across = (own, mate[0]) if where == "own" else (mate, r)
    return [c for c in pool if (topo.die(c) != topo.die(r)) == bool(far) and topo.may_write(c, across) == bool(port)][n]


def _wires(T, topo):
    members = [T.cores[r] for r in T.tables["G1"]]
    wires = []
    for r in members:
        wires.append([([_pick(topo, r, s) for s in snd], _pick(topo, r, red)) for (_w, snd, red) in LANES])
    return members, wires


def _share(k, n, f):
    ring = [(k + t) % M for t in range(M)]
    return ring[f * M // n:(f + 1) * M // n]


def _fan(g, core, topo, items, local_sem):
    batch, used, n = [], 0, 0
    for dst, s_ap, d_ap, sem in items:
        free = [e for e in _engines(topo.mask(core, dst)) if not e & used]
        if not free:
            g.remote_dma_fused(batch, local_sem=local_sem)
            batch, used = [], 0
            free = _engines(topo.mask(core, dst))
        used |= free[-1]
        rid, pid = topo.addr(dst, core)
        batch.append(RemoteDMATransfer(dst_ids=[DstId(rid=rid, pnc=pid)], dma_engine_mask=free[-1], remote_sem=sem,
                                       src=s_ap, dst=d_ap))
        n += 1
    if batch:
        g.remote_dma_fused(batch, local_sem=local_sem)
    return n


def _to_reducers(core, T, wires, k, l, pieces):
    s, r = T["s%d" % l], T["r%d" % l]
    return [(wires[j][l][1], s[j], r[k], T.sem.got) for j in pieces if wires[j][l][1] != core]


def _fold_mask(topo, red, members):
    m = topo.mask(red, members[0])
    for c in members:
        m &= topo.mask(red, c)
    return m


def _helper(g, core, T, topo, members, wires):
    S = T.sem
    sent = 0
    busy = False
    for k in range(M):
        for l in range(NL):
            snd, red = wires[k][l]
            if core in snd:
                mine = _share(k, len(snd), snd.index(core))
                g.wait_ge(S.rel, len(mine))
                sent += _fan(g, core, topo, _to_reducers(core, T, wires, k, l, mine), S.sent)
                busy = True
    for k in range(M):
        for l in range(NL):
            if wires[k][l][1] != core:
                continue
            srcs, n_in = [], 0
            for i in range(M):
                snd = wires[i][l][0]
                frm = [c for f, c in enumerate(snd) if k in _share(i, len(snd), f)][0]
                if frm == core:
                    srcs.append(T["s%d" % l][k])
                else:
                    srcs.append(T["r%d" % l][i])
                    n_in += 1
            g.wait_ge(S.got, n_in)
            mask = _fold_mask(topo, core, members)
            ring = [members[(k + 1 + t) % M] for t in range(M)]
            ids = [DstId(rid=topo.addr(c, core)[0], pnc=topo.addr(c, core)[1]) for c in ring]
            g.remote_dma_fused([RemoteDMATransfer(dst_ids=ids, dma_engine_mask=mask, remote_sem=S["arr%d" % l], srcs=srcs,
                                                  dsts=[T["r%d" % l][k] for _c in ring], alu_op=1)], local_sem=S.sent)
            sent += len(_engines(mask))
            busy = True
    if busy:
        g.wait_ge(S.sent, sent)


def _rank(g, core, T, topo, members, wires):
    S = T.sem
    k = members.index(core)
    queues = (g.sync, g.scalar)
    group2 = [T.cores[r] for r in T.tables["G2"]]
    in2 = core in group2
    me = group2.index(core) if in2 else 0
    b = T.x2.shape[1] // len(group2)
    span, row = [], 0
    for l in range(NL):
        n = M * P * LANES[l][0] // COLS
        span.append((row, row + n))
        queues[l % 2].dma_start(T["s%d" % l][:], T.x1[row:row + n, :]).then_inc(S["ld%d" % l], 16)
        row += n
    if in2:
        g.sync.dma_start(T.xs2[:], T.x2[:]).then_inc(S.l2, 16)
        g.scalar.dma_start(T.land2[:, b * me:b * me + b], T.x2[:, b * me:b * me + b]).then_inc(S.l2o, 16)
    sent = 0
    for l in range(NL):
        snd = wires[k][l][0]
        s = T["s%d" % l]
        items = []
        for f, c in enumerate(snd):
            mine = _share(k, len(snd), f)
            items += _to_reducers(core, T, wires, k, l, mine) if c == core else [(c, s[j], s[j], S.rel) for j in mine]
        g.wait_ge(S["ld%d" % l], 16)
        sent += _fan(g, core, topo, items, S.sent)
    if in2:
        g.wait_ge(S.l2, 16)
        sent += _fan(g, core, topo, [(c, T.xs2[:, b * j:b * j + b], T.land2[:, b * me:b * me + b], S.a2)
                                     for j, c in enumerate(group2) if c != core], S.sent)
    for q, lanes in zip(queues, STORES):
        for l in lanes:
            q.wait_ge(S["arr%d" % l], sum(len(_engines(_fold_mask(topo, wires[j][l][1], members))) for j in range(M)))
            q.dma_start(T.y1[span[l][0]:span[l][1], :], T["r%d" % l][:]).then_inc(S["st%d" % l], 16)
    if in2:
        g.wait_ge(S.l2o, 16)
        g.wait_ge(S.a2, len(group2) - 1)
        g.dma_start(T.y2[:], T.land2[:]).then_inc(S.sty2, 16)
        g.wait_ge(S.sty2, 16)
    g.wait_ge(S.sent, sent)
    for q, lanes in zip(queues, STORES):
        for l in lanes:
            q.wait_ge(S["st%d" % l], 16)


def rank_program(g, core, T, topo):
    members, wires = _wires(T, topo)
    if core in members:
        _rank(g, core, T, topo, members, wires)
    else:
        _helper(g, core, T, topo, members, wires)
